import numpy as np
import ml_dtypes


def mxq(x, axis, fmt="e4m3"):
    dtype, down = {"e4m3": (ml_dtypes.float8_e4m3fn, 7), "e5m2": (ml_dtypes.float8_e5m2, 14)}[fmt]
    v = np.moveaxis(np.asarray(x, np.float32).astype(ml_dtypes.bfloat16).astype(np.float64), axis, -1)
    blocks = v.reshape(v.shape[:-1] + (-1, 32))
    amax = np.abs(blocks).max(-1, keepdims=True)
    byte = np.maximum(np.where(amax > 0, np.frexp(amax)[1] - 1 + 127, 0) - down, 1)
    scale = np.exp2(byte - 127.0)
    codes = (blocks / scale).astype(np.float32).astype(dtype).astype(np.float64)
    return np.moveaxis((codes * scale).reshape(v.shape), -1, axis)


WIDE = False


def mx_kscale(k):
    if not WIDE:
        return np.ones(k)
    levels = np.array([10, -10, 5, -5, 0])
    if k % 512:
        return np.exp2(np.random.permutation(np.resize(levels, k // 32))).repeat(32)
    a = np.empty((k // 512, 16))
    for p in range(k // 512):
        a[p, :8] = np.random.permutation(np.resize(levels, 8))
        for g in range(8):
            far = levels[np.abs(levels - a[p, g]) >= 10]
            a[p, g + 8] = far[np.random.randint(len(far))]
    return np.exp2(a.ravel()).repeat(32)


def f64(x):
    return np.asarray(x).astype(np.float64)


def striped(idx):
    return np.tile(np.asarray(idx).reshape(-1, 16).T, (8, 1)).astype(np.uint16)


def unstriped(offs):
    return offs[:16].T.reshape(-1).astype(np.int64)


E2M1 = np.array([0.0, 0.5, 1.0, 1.5, 2.0, 3.0, 4.0, 6.0, -0.0, -0.5, -1.0, -1.5, -2.0, -3.0, -4.0, -6.0])


def pack_weight(w, fmt):
    k, n = w.shape
    w = f64(np.asarray(w, np.float32).astype(ml_dtypes.bfloat16)).reshape(k // 32, 32, n)
    amax = np.abs(w).max(1)
    if fmt == "e4m3":
        byte = np.frexp(amax)[1] - 1 + 127 - 7
    else:
        mant, ex = np.frexp(amax / 6.0)
        byte = np.where(mant > 0.5, ex, ex - 1) + 127
    byte = np.clip(np.where(amax > 0, byte, 1), 1, 254)
    scaled = (w * np.exp2(127.0 - byte)[:, None, :]).reshape(k, n).astype(np.float32)
    by_word = np.ascontiguousarray(scaled.reshape(k // 512, 128, 4, n).transpose(0, 1, 3, 2))
    if fmt == "e4m3":
        words = by_word.astype(ml_dtypes.float8_e4m3fn).view(np.uint8)
    else:
        c = by_word.astype(ml_dtypes.float4_e2m1fn).view(np.uint8) & 0xF
        words = (c[..., 0::2] | (c[..., 1::2] << 4)).reshape(k // 512, 128, 2 * n)
    return np.ascontiguousarray(words), np.ascontiguousarray(byte.astype(np.uint8).reshape(k // 512, 16, n))


def unpack_weight(words, scales, fmt):
    g, _, n = scales.shape
    words = np.ascontiguousarray(words).reshape(g, 128, n, -1)
    if fmt == "e4m3":
        vals = words.view(ml_dtypes.float8_e4m3fn).astype(np.float64)
    else:
        nib = np.empty((g, 128, n, 4), np.uint8)
        nib[..., 0::2] = words & 0xF
        nib[..., 1::2] = words >> 4
        vals = E2M1[nib]
    vals = vals * np.repeat(np.exp2(scales.astype(np.float64) - 127.0), 8, axis=1)[..., None]
    return vals.transpose(0, 1, 3, 2).reshape(g * 512, n)


D, T, I, Q = 512, 2048, 512, 128


def setup_inputs():
    n = np.random.standard_normal
    idx = np.random.permutation(T)[:I]
    fd = mx_kscale(D)
    keysp = pack_weight(n((D, T)) / fd[:, None], "e4m3")
    return {
        "query": (n((D, Q)) * 0.5 / np.sqrt(D) * fd[:, None]).astype(np.float32),
        "keys_words": keysp[0],
        "keys_scales": keysp[1],
        "counts": (np.random.uniform(0.0, 2.0, (Q, T))).astype(np.float32),
        "weary": (np.random.uniform(0.2, 0.8, (Q, 1))).astype(np.float32),
        "offs": striped(idx),
    }


def reference(query, keys_words, keys_scales, counts, weary, offs):
    idx = unstriped(offs)
    keysu = unpack_weight(keys_words, keys_scales, "e4m3")
    queryq = mxq(f64(query), 0, "e4m3")
    keysidxg = keysu[:, idx]
    a = queryq.T @ keysidxg
    s = a - f64(counts)[:, idx] * f64(weary)
    p = np.exp(s - np.max(s, axis=1, keepdims=True))
    w = p / np.sum(p, axis=1, keepdims=True) * 512.0
    wf = np.zeros((Q, T))
    wf[:, idx] = w
    y = f64(counts) + wf
    return y

@@ -1,0 +1,134 @@
+from contextlib import ExitStack
+
+import concourse.mybir as mybir
+
+F32 = mybir.dt.float32
+BF16 = mybir.dt.bfloat16
+I32 = mybir.dt.int32
+U32 = mybir.dt.uint32
+U16 = mybir.dt.uint16
+U8 = mybir.dt.uint8
+FP8X4 = mybir.dt.float8_e4m3fn_x4
+ALU = mybir.AluOpType
+ACT = mybir.ActivationFunctionType
+
+P = 128
+D, T, I, Q = 512, 2048, 512, 128
+PACK = 4
+HALF = I // 2
+HALF_COLS = HALF // 16
+STORE_COLS = 256
+
+FLOPS = 2 * D * I * Q
+
+
+def tile_attend_readcounts_kernel(tc, query, keys_words, keys_scales, counts, weary, offs, out):
+    nc = tc.nc
+    with ExitStack() as ctx:
+        keep = ctx.enter_context(tc.tile_pool(name="keep", bufs=1))
+        psum = ctx.enter_context(tc.psum_pool(name="psum", bufs=1))
+
+        offsets = keep.tile([P, I // 16], U16, name="offsets")
+        nc.sync.dma_start(offsets[:], offs)
+
+        pool_scales = keep.tile([P, T], U8, name="pool_scales", tag="scales_then_counts", align_bytes=64)
+        nc.vector.memset(pool_scales[:].bitcast(I32), 0)
+        for r in range(4):
+            nc.scalar.dma_start(
+                out=pool_scales[r:P:32, :].bitcast(I32),
+                in_=keys_scales[0, r:16:4, :].bitcast(I32),
+            )
+
+        q_raw = keep.tile([P, PACK, Q], F32, name="q_raw")
+        nc.sync.dma_start(out=q_raw[:], in_=query.rearrange("(p j) q -> p j q", j=PACK))
+        pool_words = keep.tile([P, T], I32, name="pool_words", align_bytes=64)
+        nc.sync.dma_start(out=pool_words[:], in_=keys_words[0].rearrange("p n t -> p (n t)").bitcast(I32))
+        pool_counts = keep.tile([P, T], F32, name="pool_counts", align_bytes=64)
+        nc.sync.dma_start(out=pool_counts[:], in_=counts)
+        weary_col = keep.tile([P, 1], F32, name="weary_col")
+        nc.scalar.dma_start(out=weary_col[:], in_=weary)
+
+        placed = keep.tile([P, T], F32, name="placed", align_bytes=64)
+        nc.vector.memset(placed[:], 0.0)
+
+        key_scales = keep.tile([P, I], U8, name="key_scales", align_bytes=64)
+        nc.vector.tensor_copy(key_scales[:], pool_scales[:].indirect(offsets[:]))
+
+        q_grouped = keep.tile([P, Q, PACK], BF16, name="q_grouped", align_bytes=64)
+        nc.vector.tensor_copy(out=q_grouped[:], in_=q_raw[:].rearrange("p j q -> p q j"))
+        q_codes = keep.tile([P, Q], U32, name="q_codes", align_bytes=64)
+        q_scales = keep.tile([P, Q], U8, name="q_scales", align_bytes=64)
+        nc.vector.quantize_mx(
+            out=q_codes[:].bitcast(FP8X4),
+            scales=q_scales[:],
+            in_=q_grouped[:].rearrange("p q j -> p (q j)"),
+        )
+
+        key_words = keep.tile([P, I], U32, name="key_words", align_bytes=64)
+        nc.vector.tensor_copy(key_words[:], pool_words[:].bitcast(U32).indirect(offsets[:]))
+
+        scores = psum.tile([P, I], F32, name="scores")
+        nc.tensor.matmul_mx(
+            out=scores[:],
+            lhsT=q_codes[:].bitcast(FP8X4),
+            lhsT_scale=q_scales[:],
+            rhs=key_words[:].bitcast(FP8X4),
+            rhs_scale=key_scales[:],
+            start=True,
+            stop=True,
+        )
+
+        halves = [slice(h * HALF, (h + 1) * HALF) for h in range(2)]
+        lists = [offsets[:, h * HALF_COLS : (h + 1) * HALF_COLS] for h in range(2)]
+
+        slot_counts = keep.tile([P, I], F32, name="slot_counts", tag="scales_then_counts", align_bytes=64)
+        for h in range(2):
+            nc.vector.tensor_copy(slot_counts[:, halves[h]], pool_counts[:].indirect(lists[h]))
+        neg_s = keep.tile([P, I], F32, name="neg_s", align_bytes=64)
+        for h in range(2):
+            nc.vector.scalar_tensor_tensor(
+                out=neg_s[:, halves[h]],
+                in0=slot_counts[:, halves[h]],
+                scalar=weary_col[:],
+                in1=scores[:, halves[h]],
+                op0=ALU.mult,
+                op1=ALU.subtract,
+            )
+        neg_max = keep.tile([P, 1], F32, name="neg_max")
+        nc.vector.tensor_reduce(out=neg_max[:], in_=neg_s[:], axis=mybir.AxisListType.X, op=ALU.min)
+
+        probs = keep.tile([P, I], F32, name="probs", align_bytes=64)
+        half_sums = keep.tile([P, 2], F32, name="half_sums")
+        for h in range(2):
+            nc.scalar.activation(
+                out=probs[:, halves[h]],
+                in_=neg_s[:, halves[h]],
+                func=ACT.Exp,
+                bias=neg_max[:],
+                scale=-1.0,
+                accum_out=half_sums[:, h : h + 1],
+            )
+        scaled_sums = keep.tile([P, 2], F32, name="scaled_sums")
+        mean_p = keep.tile([P, 1], F32, name="mean_p")
+        nc.scalar.activation(
+            out=scaled_sums[:], in_=half_sums[:], func=ACT.Copy, scale=1.0 / 512.0, accum_out=mean_p[:]
+        )
+
+        factor = keep.tile([P, 1], F32, name="factor")
+        nc.vector.tensor_copy(placed[:].indirect(lists[0]), probs[:, halves[0]])
+        nc.vector.reciprocal(factor[:], mean_p[:])
+        nc.vector.tensor_copy(placed[:].indirect(lists[1]), probs[:, halves[1]])
+
+        for c in range(T // STORE_COLS):
+            cols = slice(c * STORE_COLS, (c + 1) * STORE_COLS)
+            result = keep.tile([P, STORE_COLS], F32, name=f"result{c}", align_bytes=64)
+            nc.vector.scalar_tensor_tensor(
+                out=result[:],
+                in0=placed[:, cols],
+                scalar=factor[:],
+                in1=pool_counts[:, cols],
+                op0=ALU.mult,
+                op1=ALU.add,
+            )
+            queue = nc.sync if c % 2 == 0 else nc.scalar
+            queue.dma_start(out=out[:, cols], in_=result[:])

@@ -17,7 +17,7 @@ D, T, I, Q = 512, 2048, 512, 128
 PACK = 4
 HALF = I // 2
 HALF_COLS = HALF // 16
-STORE_COLS = 256
+STORE_WIDTHS = [160] + [288] * 6 + [160]
 
 FLOPS = 2 * D * I * Q
 
@@ -49,7 +49,7 @@ def tile_attend_readcounts_kernel(tc, query, keys_words, keys_scales, counts, we
         nc.scalar.dma_start(out=weary_col[:], in_=weary)
 
         placed = keep.tile([P, T], F32, name="placed", align_bytes=64)
-        nc.vector.memset(placed[:], 0.0)
+        nc.vector.memset(placed[:], 2.0**126)
 
         key_scales = keep.tile([P, I], U8, name="key_scales", align_bytes=64)
         nc.vector.tensor_copy(key_scales[:], pool_scales[:].indirect(offsets[:]))
@@ -95,40 +95,32 @@ def tile_attend_readcounts_kernel(tc, query, keys_words, keys_scales, counts, we
                 op1=ALU.subtract,
             )
         neg_max = keep.tile([P, 1], F32, name="neg_max")
+        nc.vector.tensor_copy(placed[:].indirect(lists[0]), neg_s[:, halves[0]])
         nc.vector.tensor_reduce(out=neg_max[:], in_=neg_s[:], axis=mybir.AxisListType.X, op=ALU.min)
+        nc.vector.tensor_copy(placed[:].indirect(lists[1]), neg_s[:, halves[1]])
 
         probs = keep.tile([P, I], F32, name="probs", align_bytes=64)
-        half_sums = keep.tile([P, 2], F32, name="half_sums")
-        for h in range(2):
-            nc.scalar.activation(
-                out=probs[:, halves[h]],
-                in_=neg_s[:, halves[h]],
-                func=ACT.Exp,
-                bias=neg_max[:],
-                scale=-1.0,
-                accum_out=half_sums[:, h : h + 1],
-            )
-        scaled_sums = keep.tile([P, 2], F32, name="scaled_sums")
-        mean_p = keep.tile([P, 1], F32, name="mean_p")
+        row_sum = keep.tile([P, 1], F32, name="row_sum")
         nc.scalar.activation(
-            out=scaled_sums[:], in_=half_sums[:], func=ACT.Copy, scale=1.0 / 512.0, accum_out=mean_p[:]
+            out=probs[:], in_=neg_s[:], func=ACT.Exp, bias=neg_max[:], scale=-1.0, accum_out=row_sum[:]
         )
-
+        mean_p = keep.tile([P, 1], F32, name="mean_p")
+        nc.scalar.activation(out=mean_p[:], in_=row_sum[:], func=ACT.Copy, scale=1.0 / 512.0)
         factor = keep.tile([P, 1], F32, name="factor")
-        nc.vector.tensor_copy(placed[:].indirect(lists[0]), probs[:, halves[0]])
         nc.vector.reciprocal(factor[:], mean_p[:])
-        nc.vector.tensor_copy(placed[:].indirect(lists[1]), probs[:, halves[1]])
 
-        for c in range(T // STORE_COLS):
-            cols = slice(c * STORE_COLS, (c + 1) * STORE_COLS)
-            result = keep.tile([P, STORE_COLS], F32, name=f"result{c}", align_bytes=64)
+        for c, width in enumerate(STORE_WIDTHS):
+            first = sum(STORE_WIDTHS[:c])
+            cols = slice(first, first + width)
+            spread = keep.tile([P, width], F32, name=f"spread{c}", align_bytes=64)
+            nc.scalar.activation(out=spread[:], in_=placed[:, cols], func=ACT.Exp, bias=neg_max[:], scale=-1.0)
+            result = keep.tile([P, width], F32, name=f"result{c}", align_bytes=64)
             nc.vector.scalar_tensor_tensor(
                 out=result[:],
-                in0=placed[:, cols],
+                in0=spread[:],
                 scalar=factor[:],
                 in1=pool_counts[:, cols],
                 op0=ALU.mult,
                 op1=ALU.add,
             )
-            queue = nc.sync if c % 2 == 0 else nc.scalar
-            queue.dma_start(out=out[:, cols], in_=result[:])
+            nc.sync.dma_start(out=out[:, cols], in_=result[:])

from contextlib import ExitStack

import concourse.mybir as mybir

F32 = mybir.dt.float32
BF16 = mybir.dt.bfloat16
I32 = mybir.dt.int32
U32 = mybir.dt.uint32
U16 = mybir.dt.uint16
U8 = mybir.dt.uint8
FP8X4 = mybir.dt.float8_e4m3fn_x4
ALU = mybir.AluOpType
ACT = mybir.ActivationFunctionType

P = 128
D, T, I, Q = 512, 2048, 512, 128
PACK = 4
HALF = I // 2
HALF_COLS = HALF // 16
STORE_WIDTHS = [160] + [288] * 6 + [160]

FLOPS = 2 * D * I * Q


def tile_attend_readcounts_kernel(tc, query, keys_words, keys_scales, counts, weary, offs, out):
    nc = tc.nc
    with ExitStack() as ctx:
        keep = ctx.enter_context(tc.tile_pool(name="keep", bufs=1))
        psum = ctx.enter_context(tc.psum_pool(name="psum", bufs=1))

        offsets = keep.tile([P, I // 16], U16, name="offsets")
        nc.sync.dma_start(offsets[:], offs)

        pool_scales = keep.tile([P, T], U8, name="pool_scales", tag="scales_then_counts", align_bytes=64)
        nc.vector.memset(pool_scales[:].bitcast(I32), 0)
        for r in range(4):
            nc.scalar.dma_start(
                out=pool_scales[r:P:32, :].bitcast(I32),
                in_=keys_scales[0, r:16:4, :].bitcast(I32),
            )

        q_raw = keep.tile([P, PACK, Q], F32, name="q_raw")
        nc.sync.dma_start(out=q_raw[:], in_=query.rearrange("(p j) q -> p j q", j=PACK))
        pool_words = keep.tile([P, T], I32, name="pool_words", align_bytes=64)
        nc.sync.dma_start(out=pool_words[:], in_=keys_words[0].rearrange("p n t -> p (n t)").bitcast(I32))
        pool_counts = keep.tile([P, T], F32, name="pool_counts", align_bytes=64)
        nc.sync.dma_start(out=pool_counts[:], in_=counts)
        weary_col = keep.tile([P, 1], F32, name="weary_col")
        nc.scalar.dma_start(out=weary_col[:], in_=weary)

        placed = keep.tile([P, T], F32, name="placed", align_bytes=64)
        nc.vector.memset(placed[:], 2.0**126)

        key_scales = keep.tile([P, I], U8, name="key_scales", align_bytes=64)
        nc.vector.tensor_copy(key_scales[:], pool_scales[:].indirect(offsets[:]))

        q_grouped = keep.tile([P, Q, PACK], BF16, name="q_grouped", align_bytes=64)
        nc.vector.tensor_copy(out=q_grouped[:], in_=q_raw[:].rearrange("p j q -> p q j"))
        q_codes = keep.tile([P, Q], U32, name="q_codes", align_bytes=64)
        q_scales = keep.tile([P, Q], U8, name="q_scales", align_bytes=64)
        nc.vector.quantize_mx(
            out=q_codes[:].bitcast(FP8X4),
            scales=q_scales[:],
            in_=q_grouped[:].rearrange("p q j -> p (q j)"),
        )

        key_words = keep.tile([P, I], U32, name="key_words", align_bytes=64)
        nc.vector.tensor_copy(key_words[:], pool_words[:].bitcast(U32).indirect(offsets[:]))

        scores = psum.tile([P, I], F32, name="scores")
        nc.tensor.matmul_mx(
            out=scores[:],
            lhsT=q_codes[:].bitcast(FP8X4),
            lhsT_scale=q_scales[:],
            rhs=key_words[:].bitcast(FP8X4),
            rhs_scale=key_scales[:],
            start=True,
            stop=True,
        )

        halves = [slice(h * HALF, (h + 1) * HALF) for h in range(2)]
        lists = [offsets[:, h * HALF_COLS : (h + 1) * HALF_COLS] for h in range(2)]

        slot_counts = keep.tile([P, I], F32, name="slot_counts", tag="scales_then_counts", align_bytes=64)
        for h in range(2):
            nc.vector.tensor_copy(slot_counts[:, halves[h]], pool_counts[:].indirect(lists[h]))
        neg_s = keep.tile([P, I], F32, name="neg_s", align_bytes=64)
        for h in range(2):
            nc.vector.scalar_tensor_tensor(
                out=neg_s[:, halves[h]],
                in0=slot_counts[:, halves[h]],
                scalar=weary_col[:],
                in1=scores[:, halves[h]],
                op0=ALU.mult,
                op1=ALU.subtract,
            )
        neg_max = keep.tile([P, 1], F32, name="neg_max")
        nc.vector.tensor_copy(placed[:].indirect(lists[0]), neg_s[:, halves[0]])
        nc.vector.tensor_reduce(out=neg_max[:], in_=neg_s[:], axis=mybir.AxisListType.X, op=ALU.min)
        nc.vector.tensor_copy(placed[:].indirect(lists[1]), neg_s[:, halves[1]])

        probs = keep.tile([P, I], F32, name="probs", align_bytes=64)
        row_sum = keep.tile([P, 1], F32, name="row_sum")
        nc.scalar.activation(
            out=probs[:], in_=neg_s[:], func=ACT.Exp, bias=neg_max[:], scale=-1.0, accum_out=row_sum[:]
        )
        mean_p = keep.tile([P, 1], F32, name="mean_p")
        nc.scalar.activation(out=mean_p[:], in_=row_sum[:], func=ACT.Copy, scale=1.0 / 512.0)
        factor = keep.tile([P, 1], F32, name="factor")
        nc.vector.reciprocal(factor[:], mean_p[:])

        for c, width in enumerate(STORE_WIDTHS):
            first = sum(STORE_WIDTHS[:c])
            cols = slice(first, first + width)
            spread = keep.tile([P, width], F32, name=f"spread{c}", align_bytes=64)
            nc.scalar.activation(out=spread[:], in_=placed[:, cols], func=ACT.Exp, bias=neg_max[:], scale=-1.0)
            result = keep.tile([P, width], F32, name=f"result{c}", align_bytes=64)
            nc.vector.scalar_tensor_tensor(
                out=result[:],
                in0=spread[:],
                scalar=factor[:],
                in1=pool_counts[:, cols],
                op0=ALU.mult,
                op1=ALU.add,
            )
            nc.sync.dma_start(out=out[:, cols], in_=result[:])
